import numpy as np
import ml_dtypes


def mxq(x, axis, fmt="e4m3"):
    dtype, down = {"e4m3": (ml_dtypes.float8_e4m3fn, 7), "e5m2": (ml_dtypes.float8_e5m2, 14)}[fmt]
    v = np.moveaxis(np.asarray(x, np.float32).astype(ml_dtypes.bfloat16).astype(np.float64), axis, -1)
    blocks = v.reshape(v.shape[:-1] + (-1, 32))
    amax = np.abs(blocks).max(-1, keepdims=True)
    byte = np.maximum(np.where(amax > 0, np.frexp(amax)[1] - 1 + 127, 0) - down, 1)
    scale = np.exp2(byte - 127.0)
    codes = (blocks / scale).astype(np.float32).astype(dtype).astype(np.float64)
    return np.moveaxis((codes * scale).reshape(v.shape), -1, axis)


WIDE = False


def mx_kscale(k):
    if not WIDE:
        return np.ones(k)
    levels = np.array([24, -24, 12, -12, 0])
    if k % 512:
        return np.exp2(np.random.permutation(np.resize(levels, k // 32))).repeat(32)
    a = np.empty((k // 512, 16))
    for p in range(k // 512):
        a[p, :8] = np.random.permutation(np.resize(levels, 8))
        for g in range(8):
            far = levels[np.abs(levels - a[p, g]) >= 10]
            a[p, g + 8] = far[np.random.randint(len(far))]
    return np.exp2(a.ravel()).repeat(32)


def f64(x):
    return np.asarray(x).astype(np.float64)


def striped8(idx):
    return np.concatenate([v.reshape(-1, 16).T for v in idx]).astype(np.uint16)


def unstriped8(offs):
    return np.stack([offs[16 * g:16 * g + 16].T.reshape(-1) for g in range(8)]).astype(np.int64)


def split(x):
    m, e = np.frexp(f64(x))
    hi = np.ldexp(np.trunc(16.0 * m) / 16.0, e)
    return hi, f64(x) - hi


def sigm(f):
    return 1.0 / (1.0 + np.exp(-np.maximum(f, -700.0)))


K, L, N, T, J = 512, 512, 512, 2048, 1024


def setup_inputs():
    n = np.random.standard_normal
    s = mx_kscale(K)[:, None]
    s2 = mx_kscale(L)[:, None]
    return {
        "xT": (n((K, T)) * s).astype(np.float32),
        "wgt": np.repeat(np.random.uniform(0.5, 2.0, (8, J)), 16, axis=0).astype(np.float32),
        "zT": (n((L, T)) * s2).astype(np.float32),
        "wgt2": np.repeat(np.random.uniform(0.5, 2.0, (8, J)), 16, axis=0).astype(np.float32),
        "wa": (n((K, N)) / np.sqrt(K) / s).astype(np.float32),
        "wb": (n((L, N)) / np.sqrt(L) / s2).astype(np.float32),
        "res": (n((N, J))).astype(np.float32),
        "offs": striped8(np.stack([np.random.permutation(T)[:J] for _ in range(8)])),
        "offs2": striped8(np.stack([np.random.permutation(T)[:J] for _ in range(8)])),
    }


def reference(xT, wgt, zT, wgt2, wa, wb, res, offs, offs2):
    idx = unstriped8(offs)
    idx2 = unstriped8(offs2)
    rows = np.arange(K)
    xg = f64(wgt)[rows // 4 % 128] * f64(xT)[rows[:, None], idx[rows % 512 // 64]]
    xT_ = mxq(xg, 0, "e4m3")
    rows = np.arange(L)
    xg = f64(wgt2)[rows // 4 % 128] * f64(zT)[rows[:, None], idx2[rows % 512 // 64]]
    zT_ = mxq(xg, 0, "e4m3")
    wa_ = mxq(f64(wa), 0, "e4m3")
    wb_hi, wb_lo = split(wb)
    wb_hi_, wb_lo_ = mxq(wb_hi, 0, "e4m3"), mxq(wb_lo, 0, "e4m3")
    ya = wa_.T @ xT_
    yb = wb_hi_.T @ zT_ + wb_lo_.T @ zT_
    return ya * sigm(yb) + f64(res)

@@ -1,0 +1,154 @@
+from contextlib import ExitStack
+
+import concourse.mybir as mybir
+
+K, L, N, T, J = 512, 512, 512, 2048, 1024
+FLOPS = 2 * N * J * (K + 2 * L)
+
+F32 = mybir.dt.float32
+BF16 = mybir.dt.bfloat16
+I32 = mybir.dt.int32
+U32 = mybir.dt.uint32
+U16 = mybir.dt.uint16
+U8 = mybir.dt.uint8
+FP8X4 = mybir.dt.float8_e4m3fn_x4
+ALU = mybir.AluOpType
+ACT = mybir.ActivationFunctionType
+
+P = 128
+PACK = 4
+N_TILES = N // P
+CHUNK = 256
+CHUNKS = J // CHUNK
+HI_MASK = -(1 << 20)
+
+
+def interleave(nc, dst, src):
+    nc.scalar.copy(
+        out=dst.rearrange("p (c e) i -> p c i e", e=4),
+        in_=src.rearrange("p i (c e) -> p c i e", e=4),
+    )
+
+
+def quantize(nc, codes, scales, grouped):
+    nc.vector.quantize_mx(out=codes.bitcast(FP8X4), scales=scales, in_=grouped.rearrange("p c i -> p (c i)"))
+
+
+def tile_list_hl_gate_res_kernel(tc, xT, wgt, zT, wgt2, wa, wb, res, offs, offs2, out):
+    nc = tc.nc
+    with ExitStack() as ctx:
+        keep = ctx.enter_context(tc.tile_pool(name="keep", bufs=1))
+        ring = ctx.enter_context(tc.tile_pool(name="ring", bufs=2))
+        psum = ctx.enter_context(tc.psum_pool(name="psum", bufs=4))
+
+        x_offs = keep.tile([P, J // 16], U16, name="x_offs")
+        z_offs = keep.tile([P, J // 16], U16, name="z_offs")
+        x_wgt = keep.tile([P, J], F32, name="x_wgt")
+        z_wgt = keep.tile([P, J], F32, name="z_wgt")
+        x_planes = [keep.tile([P, T], F32, name="x_plane%d" % i) for i in range(PACK)]
+        z_planes = [keep.tile([P, T], F32, name="z_plane%d" % i) for i in range(PACK)]
+        wa_raw = keep.tile([P, PACK, N], F32, name="wa_raw")
+        wb_raw = keep.tile([P, PACK, N], F32, name="wb_raw")
+        res_sb = [keep.tile([P, N_TILES, J // 2], F32, name="res%d" % h) for h in range(2)]
+
+        x_rows = xT.rearrange("(p i) t -> p i t", i=PACK)
+        z_rows = zT.rearrange("(p i) t -> p i t", i=PACK)
+        wb_rows = wb.rearrange("(p i) n -> p i n", i=PACK)
+        res_rows = res.rearrange("(t p) j -> p t j", p=P)
+        out_rows = out.rearrange("(t p) j -> p t j", p=P)
+
+        for h in range(2):
+            nc.sync.dma_start(out=wb_raw[:, 2 * h : 2 * h + 2, :], in_=wb_rows[:, 2 * h : 2 * h + 2, :])
+        nc.sync.dma_start(z_offs[:], offs2)
+        nc.sync.dma_start(out=z_planes[0][:], in_=z_rows[:, 0, :])
+        nc.sync.dma_start(out=z_wgt[:], in_=wgt2)
+        for i in range(1, PACK):
+            nc.sync.dma_start(out=z_planes[i][:], in_=z_rows[:, i, :])
+        nc.sync.dma_start(x_offs[:], offs)
+        nc.sync.dma_start(out=x_wgt[:], in_=wgt)
+        nc.sync.dma_start(out=x_planes[0][:], in_=x_rows[:, 0, :])
+        nc.sync.dma_start(out=wa_raw[:], in_=wa.rearrange("(p i) n -> p i n", i=PACK))
+        for i in range(1, PACK):
+            nc.sync.dma_start(out=x_planes[i][:], in_=x_rows[:, i, :])
+        for h in range(2):
+            nc.sync.dma_start(out=res_sb[h][:], in_=res_rows[:, :, h * (J // 2) : (h + 1) * (J // 2)])
+
+        wb_hi = keep.tile([P, PACK, N], F32, name="wb_hi")
+        wb_lo = keep.tile([P, PACK, N], BF16, name="wb_lo")
+        for h in range(2):
+            rows = slice(2 * h, 2 * h + 2)
+            nc.vector.tensor_scalar(
+                out=wb_hi[:, rows, :].bitcast(I32), in0=wb_raw[:, rows, :].bitcast(I32),
+                scalar1=HI_MASK, scalar2=None, op0=ALU.bitwise_and,
+            )
+        for h in range(2):
+            rows = slice(2 * h, 2 * h + 2)
+            nc.vector.tensor_tensor(out=wb_lo[:, rows, :], in0=wb_raw[:, rows, :], in1=wb_hi[:, rows, :], op=ALU.subtract)
+
+        weights = {}
+        for name, raw in (("hi", wb_hi), ("lo", wb_lo), ("wa", wa_raw)):
+            grouped = keep.tile([P, N, PACK], BF16, name="grouped_" + name, align_bytes=64)
+            codes = keep.tile([P, N], U32, name="codes_" + name, align_bytes=64)
+            scales = keep.tile([P, N], U8, name="scales_" + name, align_bytes=64)
+            interleave(nc, grouped[:], raw[:])
+            quantize(nc, codes[:], scales[:], grouped[:])
+            weights[name] = (codes, scales)
+
+        def product(bank, name, t, codes, scales, start, stop):
+            w_codes, w_scales = weights[name]
+            cols = slice(t * P, (t + 1) * P)
+            nc.tensor.matmul_mx(
+                out=bank, lhsT=w_codes[:, cols].bitcast(FP8X4), lhsT_scale=w_scales[:, cols],
+                rhs=codes[:].bitcast(FP8X4), rhs_scale=scales[:], start=start, stop=stop,
+            )
+
+        def picked_chunks(name, planes, offsets, weight):
+            picked = keep.tile([P, PACK, J], F32, name="picked_" + name)
+            for i in range(PACK - 1):
+                nc.vector.tensor_tensor(picked[:, i, :], planes[i][:].indirect(offsets[:]), weight[:], ALU.mult)
+            made = []
+            for c in range(CHUNKS):
+                cols = slice(c * CHUNK, (c + 1) * CHUNK)
+                nc.vector.tensor_tensor(
+                    picked[:, PACK - 1, cols],
+                    planes[PACK - 1][:].indirect(offsets[:, c * CHUNK // 16 : (c + 1) * CHUNK // 16]),
+                    weight[:, cols], ALU.mult,
+                )
+            for c in range(CHUNKS):
+                cols = slice(c * CHUNK, (c + 1) * CHUNK)
+                grouped = keep.tile([P, CHUNK, PACK], BF16, name="grouped_%s%d" % (name, c), align_bytes=64)
+                codes = keep.tile([P, CHUNK], U32, name="codes_%s%d" % (name, c), align_bytes=64)
+                scales = keep.tile([P, CHUNK], U8, name="scales_%s%d" % (name, c), align_bytes=64)
+                interleave(nc, grouped[:], picked[:, :, cols])
+                quantize(nc, codes[:], scales[:], grouped[:])
+                made.append((codes, scales))
+            return made
+
+        gates = []
+        for c, (codes, scales) in enumerate(picked_chunks("z", z_planes, z_offs, z_wgt)):
+            gate = keep.tile([P, N_TILES, CHUNK], F32, name="gate%d" % c)
+            for b in range(2):
+                bank = psum.tile([P, 2, CHUNK], F32, name="yb")
+                for u in range(2):
+                    product(bank[:, u, :], "hi", 2 * b + u, codes, scales, True, False)
+                    product(bank[:, u, :], "lo", 2 * b + u, codes, scales, False, True)
+                nc.scalar.activation(out=gate[:, 2 * b : 2 * b + 2, :], in_=bank[:], func=ACT.Sigmoid)
+            gates.append(gate)
+
+        for c, (codes, scales) in enumerate(picked_chunks("x", x_planes, x_offs, x_wgt)):
+            gated = ring.tile([P, N_TILES, CHUNK], F32, name="gated")
+            result = ring.tile([P, N_TILES, CHUNK], F32, name="result")
+            for b in range(2):
+                bank = psum.tile([P, 2, CHUNK], F32, name="ya")
+                for u in range(2):
+                    product(bank[:, u, :], "wa", 2 * b + u, codes, scales, True, True)
+                nc.vector.tensor_tensor(
+                    out=gated[:, 2 * b : 2 * b + 2, :], in0=bank[:], in1=gates[c][:, 2 * b : 2 * b + 2, :], op=ALU.mult
+                )
+            h, c0 = divmod(c * CHUNK, J // 2)
+            for b in range(2):
+                pair = slice(2 * b, 2 * b + 2)
+                nc.vector.tensor_tensor(
+                    out=result[:, pair, :], in0=gated[:, pair, :], in1=res_sb[h][:, pair, c0 : c0 + CHUNK], op=ALU.add
+                )
+            nc.sync.dma_start(out=out_rows[:, :, c * CHUNK : (c + 1) * CHUNK], in_=result[:])

@@ -18,8 +18,9 @@ ACT = mybir.ActivationFunctionType
 P = 128
 PACK = 4
 N_TILES = N // P
-CHUNK = 256
-CHUNKS = J // CHUNK
+X_CUTS = (0, 256, 512, 768, 1024)
+BANK = 512
+GPSIMD_PIECES = 2
 HI_MASK = -(1 << 20)
 
 
@@ -38,18 +39,17 @@ def tile_list_hl_gate_res_kernel(tc, xT, wgt, zT, wgt2, wa, wb, res, offs, offs2
     nc = tc.nc
     with ExitStack() as ctx:
         keep = ctx.enter_context(tc.tile_pool(name="keep", bufs=1))
-        ring = ctx.enter_context(tc.tile_pool(name="ring", bufs=2))
         psum = ctx.enter_context(tc.psum_pool(name="psum", bufs=4))
 
         x_offs = keep.tile([P, J // 16], U16, name="x_offs")
         z_offs = keep.tile([P, J // 16], U16, name="z_offs")
-        x_wgt = keep.tile([P, J], F32, name="x_wgt")
+        x_wgt = keep.tile([P, J], F32, name="x_wgt", align_bytes=64)
         z_wgt = keep.tile([P, J], F32, name="z_wgt")
-        x_planes = [keep.tile([P, T], F32, name="x_plane%d" % i) for i in range(PACK)]
-        z_planes = [keep.tile([P, T], F32, name="z_plane%d" % i) for i in range(PACK)]
-        wa_raw = keep.tile([P, PACK, N], F32, name="wa_raw")
-        wb_raw = keep.tile([P, PACK, N], F32, name="wb_raw")
-        res_sb = [keep.tile([P, N_TILES, J // 2], F32, name="res%d" % h) for h in range(2)]
+        x_planes = [keep.tile([P, T], F32, name="x_plane%d" % i, align_bytes=64) for i in range(PACK)]
+        z_planes = [keep.tile([P, T], F32, name="z_plane%d" % i, align_bytes=64) for i in range(PACK)]
+        wa_raw = keep.tile([P, PACK, N], F32, name="wa_raw", align_bytes=64)
+        wb_raw = [keep.tile([P, PACK, N // 2], F32, name="wb_raw%d" % h) for h in range(2)]
+        res_sb = keep.tile([P, N_TILES, J], F32, name="res_sb")
 
         x_rows = xT.rearrange("(p i) t -> p i t", i=PACK)
         z_rows = zT.rearrange("(p i) t -> p i t", i=PACK)
@@ -57,98 +57,129 @@ def tile_list_hl_gate_res_kernel(tc, xT, wgt, zT, wgt2, wa, wb, res, offs, offs2
         res_rows = res.rearrange("(t p) j -> p t j", p=P)
         out_rows = out.rearrange("(t p) j -> p t j", p=P)
 
-        for h in range(2):
-            nc.sync.dma_start(out=wb_raw[:, 2 * h : 2 * h + 2, :], in_=wb_rows[:, 2 * h : 2 * h + 2, :])
+        for r in range(0, PACK, 2):
+            nc.sync.dma_start(out=wb_raw[0][:, r : r + 2, :], in_=wb_rows[:, r : r + 2, : N // 2])
+        nc.sync.dma_start(out=wb_raw[1][:], in_=wb_rows[:, :, N // 2 :])
         nc.sync.dma_start(z_offs[:], offs2)
         nc.sync.dma_start(out=z_planes[0][:], in_=z_rows[:, 0, :])
-        nc.sync.dma_start(out=z_wgt[:], in_=wgt2)
+        for h in range(2):
+            nc.sync.dma_start(out=z_wgt[:, h * (J // 2) : (h + 1) * (J // 2)], in_=wgt2[:, h * (J // 2) : (h + 1) * (J // 2)])
         for i in range(1, PACK):
             nc.sync.dma_start(out=z_planes[i][:], in_=z_rows[:, i, :])
         nc.sync.dma_start(x_offs[:], offs)
         nc.sync.dma_start(out=x_wgt[:], in_=wgt)
-        nc.sync.dma_start(out=x_planes[0][:], in_=x_rows[:, 0, :])
+        for i in range(2):
+            nc.sync.dma_start(out=x_planes[i][:], in_=x_rows[:, i, :])
         nc.sync.dma_start(out=wa_raw[:], in_=wa.rearrange("(p i) n -> p i n", i=PACK))
-        for i in range(1, PACK):
+        for i in range(2, PACK):
             nc.sync.dma_start(out=x_planes[i][:], in_=x_rows[:, i, :])
         for h in range(2):
-            nc.sync.dma_start(out=res_sb[h][:], in_=res_rows[:, :, h * (J // 2) : (h + 1) * (J // 2)])
+            cols = slice(h * (J // 2), (h + 1) * (J // 2))
+            nc.sync.dma_start(out=res_sb[:, :, cols], in_=res_rows[:, :, cols])
 
-        wb_hi = keep.tile([P, PACK, N], F32, name="wb_hi")
-        wb_lo = keep.tile([P, PACK, N], BF16, name="wb_lo")
-        for h in range(2):
-            rows = slice(2 * h, 2 * h + 2)
-            nc.vector.tensor_scalar(
-                out=wb_hi[:, rows, :].bitcast(I32), in0=wb_raw[:, rows, :].bitcast(I32),
-                scalar1=HI_MASK, scalar2=None, op0=ALU.bitwise_and,
-            )
-        for h in range(2):
-            rows = slice(2 * h, 2 * h + 2)
-            nc.vector.tensor_tensor(out=wb_lo[:, rows, :], in0=wb_raw[:, rows, :], in1=wb_hi[:, rows, :], op=ALU.subtract)
-
-        weights = {}
-        for name, raw in (("hi", wb_hi), ("lo", wb_lo), ("wa", wa_raw)):
-            grouped = keep.tile([P, N, PACK], BF16, name="grouped_" + name, align_bytes=64)
-            codes = keep.tile([P, N], U32, name="codes_" + name, align_bytes=64)
-            scales = keep.tile([P, N], U8, name="scales_" + name, align_bytes=64)
-            interleave(nc, grouped[:], raw[:])
+        def quantized(name, grouped, tag):
+            width = grouped.shape[1]
+            codes = keep.tile([P, width], U32, name="codes_" + name, tag=tag, align_bytes=64)
+            scales = keep.tile([P, width], U8, name="scales_" + name, align_bytes=64)
             quantize(nc, codes[:], scales[:], grouped[:])
-            weights[name] = (codes, scales)
+            return codes, scales
 
-        def product(bank, name, t, codes, scales, start, stop):
-            w_codes, w_scales = weights[name]
-            cols = slice(t * P, (t + 1) * P)
+        def interleaved(name, sources):
+            width = sources[0].shape[2]
+            grouped = keep.tile([P, len(sources) * width, PACK], BF16, name="grouped_" + name, align_bytes=64)
+            for s, src in enumerate(sources):
+                interleave(nc, grouped[:, s * width : (s + 1) * width, :], src)
+            return grouped
+
+        def product(bank, weight, col, moving, start, stop):
             nc.tensor.matmul_mx(
-                out=bank, lhsT=w_codes[:, cols].bitcast(FP8X4), lhsT_scale=w_scales[:, cols],
-                rhs=codes[:].bitcast(FP8X4), rhs_scale=scales[:], start=start, stop=stop,
+                out=bank, lhsT=weight[0][:, col : col + P].bitcast(FP8X4), lhsT_scale=weight[1][:, col : col + P],
+                rhs=moving[0][:].bitcast(FP8X4), rhs_scale=moving[1][:], start=start, stop=stop,
             )
 
-        def picked_chunks(name, planes, offsets, weight):
-            picked = keep.tile([P, PACK, J], F32, name="picked_" + name)
-            for i in range(PACK - 1):
-                nc.vector.tensor_tensor(picked[:, i, :], planes[i][:].indirect(offsets[:]), weight[:], ALU.mult)
-            made = []
-            for c in range(CHUNKS):
-                cols = slice(c * CHUNK, (c + 1) * CHUNK)
-                nc.vector.tensor_tensor(
-                    picked[:, PACK - 1, cols],
-                    planes[PACK - 1][:].indirect(offsets[:, c * CHUNK // 16 : (c + 1) * CHUNK // 16]),
-                    weight[:, cols], ALU.mult,
-                )
-            for c in range(CHUNKS):
-                cols = slice(c * CHUNK, (c + 1) * CHUNK)
-                grouped = keep.tile([P, CHUNK, PACK], BF16, name="grouped_%s%d" % (name, c), align_bytes=64)
-                codes = keep.tile([P, CHUNK], U32, name="codes_%s%d" % (name, c), align_bytes=64)
-                scales = keep.tile([P, CHUNK], U8, name="scales_%s%d" % (name, c), align_bytes=64)
-                interleave(nc, grouped[:], picked[:, :, cols])
-                quantize(nc, codes[:], scales[:], grouped[:])
-                made.append((codes, scales))
-            return made
+        def gather(values, plane, offsets, weight, cols):
+            nc.vector.tensor_tensor(
+                values[:, cols], plane[:].indirect(offsets[:, cols.start // 16 : cols.stop // 16]),
+                weight[:, cols], ALU.mult,
+            )
 
-        gates = []
-        for c, (codes, scales) in enumerate(picked_chunks("z", z_planes, z_offs, z_wgt)):
-            gate = keep.tile([P, N_TILES, CHUNK], F32, name="gate%d" % c)
-            for b in range(2):
-                bank = psum.tile([P, 2, CHUNK], F32, name="yb")
-                for u in range(2):
-                    product(bank[:, u, :], "hi", 2 * b + u, codes, scales, True, False)
-                    product(bank[:, u, :], "lo", 2 * b + u, codes, scales, False, True)
-                nc.scalar.activation(out=gate[:, 2 * b : 2 * b + 2, :], in_=bank[:], func=ACT.Sigmoid)
-            gates.append(gate)
+        wb_grouped = []
+        for h in range(2):
+            wb_hi = keep.tile([P, PACK, N // 2], F32, name="wb_hi%d" % h)
+            wb_lo = keep.tile([P, PACK, N // 2], BF16, name="wb_lo%d" % h)
+            step = 2 if h == 0 else PACK
+            for r in range(0, PACK, step):
+                rows = slice(r, r + step)
+                nc.vector.tensor_scalar(
+                    out=wb_hi[:, rows, :].bitcast(I32), in0=wb_raw[h][:, rows, :].bitcast(I32),
+                    scalar1=HI_MASK, scalar2=None, op0=ALU.bitwise_and,
+                )
+            for r in range(0, PACK, step):
+                rows = slice(r, r + step)
+                nc.vector.tensor_tensor(
+                    out=wb_lo[:, rows, :], in0=wb_raw[h][:, rows, :], in1=wb_hi[:, rows, :], op=ALU.subtract
+                )
+            wb_grouped.append(interleaved("wb%d" % h, [wb_hi[:], wb_lo[:]]))
 
-        for c, (codes, scales) in enumerate(picked_chunks("x", x_planes, x_offs, x_wgt)):
-            gated = ring.tile([P, N_TILES, CHUNK], F32, name="gated")
-            result = ring.tile([P, N_TILES, CHUNK], F32, name="result")
-            for b in range(2):
-                bank = psum.tile([P, 2, CHUNK], F32, name="ya")
+        wb_mx = [quantized("wb0", wb_grouped[0], "codes_wb0")]
+        z_picked = keep.tile([P, PACK, J], F32, name="picked_z")
+        for i, width in enumerate((J // 2, J, J, J // 2)):
+            for c0 in range(0, J, width):
+                gather(z_picked[:, i, :], z_planes[i], z_offs, z_wgt, slice(c0, c0 + width))
+        wb_mx.append(quantized("wb1", wb_grouped[1], "codes_wb1"))
+        z_grouped = [interleaved("z%d" % h, [z_picked[:, :, h * (J // 2) : (h + 1) * (J // 2)]]) for h in range(2)]
+        x_picked = keep.tile([P, PACK, J], F32, name="picked_x", align_bytes=64)
+        for i in range(PACK - 1):
+            gather(x_picked[:, i, :], x_planes[i], x_offs, x_wgt, slice(0, J))
+
+        z_mx = [quantized("z%d" % h, z_grouped[h], "x_plane%d" % h) for h in range(2)]
+
+        gates = {}
+
+        def gate_rows(h, halves, tag):
+            gate = keep.tile([P, 2 * len(halves), J // 2], F32, name="gate%d%d" % (h, halves[0]), tag=tag, align_bytes=64)
+            for e, half in enumerate(halves):
                 for u in range(2):
-                    product(bank[:, u, :], "wa", 2 * b + u, codes, scales, True, True)
-                nc.vector.tensor_tensor(
-                    out=gated[:, 2 * b : 2 * b + 2, :], in0=bank[:], in1=gates[c][:, 2 * b : 2 * b + 2, :], op=ALU.mult
-                )
-            h, c0 = divmod(c * CHUNK, J // 2)
-            for b in range(2):
-                pair = slice(2 * b, 2 * b + 2)
-                nc.vector.tensor_tensor(
-                    out=result[:, pair, :], in0=gated[:, pair, :], in1=res_sb[h][:, pair, c0 : c0 + CHUNK], op=ALU.add
-                )
-            nc.sync.dma_start(out=out_rows[:, :, c * CHUNK : (c + 1) * CHUNK], in_=result[:])
+                    bank = psum.tile([P, J // 2], F32, name="yb")
+                    product(bank[:], wb_mx[half], u * P, z_mx[h], True, False)
+                    product(bank[:], wb_mx[half], N // 2 + u * P, z_mx[h], False, True)
+                    nc.scalar.activation(out=gate[:, 2 * e + u, :], in_=bank[:], func=ACT.Sigmoid)
+                gates[h, half] = gate[:, 2 * e : 2 * e + 2, :]
+
+        wa_grouped = interleaved("wa", [wa_raw[:]])
+        gate_rows(0, (0, 1), "wa_raw")
+        gate_rows(1, (0,), "gate10")
+
+        chunks = [slice(c0, c1) for c0, c1 in zip(X_CUTS, X_CUTS[1:])]
+        x_grouped = []
+        for c, cols in enumerate(chunks):
+            gather(x_picked[:, PACK - 1, :], x_planes[PACK - 1], x_offs, x_wgt, cols)
+            x_grouped.append(interleaved("x%d" % c, [x_picked[:, :, cols]]))
+        wa_mx = quantized("wa", wa_grouped, "x_plane3")
+        x_mx = [quantized("x%d" % c, grouped, "codes_x%d" % c) for c, grouped in enumerate(x_grouped)]
+        gate_rows(1, (1,), "picked_x")
+
+        pieces = []
+        for c, cols in enumerate(chunks):
+            width = cols.stop - cols.start
+            for t0 in range(0, N_TILES, BANK // width):
+                rows = slice(t0, t0 + BANK // width)
+                bank = psum.tile([P, BANK // width, width], F32, name="ya")
+                for u in range(BANK // width):
+                    product(bank[:, u, :], wa_mx, (t0 + u) * P, x_mx[c], True, True)
+                gated = keep.tile([P, BANK // width, width], F32, name="gated%d_%d" % (c, t0))
+                h, c0 = divmod(cols.start, J // 2)
+                assert c0 + width <= J // 2
+                nc.vector.tensor_tensor(out=gated[:], in0=bank[:], in1=gates[h, t0 // 2][:, :, c0 : c0 + width], op=ALU.mult)
+                pieces.append((gated, rows, cols))
+
+        first = keep.tile([P, GPSIMD_PIECES, BANK], F32, name="first", tag="grouped_x%d" % (len(chunks) - 1), align_bytes=64)
+        for e, (gated, rows, cols) in enumerate(pieces):
+            if e < GPSIMD_PIECES:
+                result = first[:, e, :].rearrange("p (u j) -> p u j", u=rows.stop - rows.start)
+                nc.gpsimd.tensor_tensor(out=result, in0=gated[:], in1=res_sb[:, rows, cols], op=ALU.add)
+                nc.scalar.dma_start(out=out_rows[:, rows, cols], in_=result)
+            else:
+                result = keep.tile(gated.shape, F32, name="result%d" % e)
+                nc.vector.tensor_tensor(out=result[:], in0=gated[:], in1=res_sb[:, rows, cols], op=ALU.add)
+                nc.sync.dma_start(out=out_rows[:, rows, cols], in_=result[:])

@@ -1,6 +1,7 @@
 from contextlib import ExitStack
 
 import concourse.mybir as mybir
+from concourse.masks import make_identity
 
 K, L, N, T, J = 512, 512, 512, 2048, 1024
 FLOPS = 2 * N * J * (K + 2 * L)
@@ -20,6 +21,7 @@ PACK = 4
 N_TILES = N // P
 X_CUTS = (0, 256, 512, 768, 1024)
 BANK = 512
+WB_CUTS = (0, 1, 2, 3, 4)
 GPSIMD_PIECES = 2
 HI_MASK = -(1 << 20)
 
@@ -48,7 +50,7 @@ def tile_list_hl_gate_res_kernel(tc, xT, wgt, zT, wgt2, wa, wb, res, offs, offs2
         x_planes = [keep.tile([P, T], F32, name="x_plane%d" % i, align_bytes=64) for i in range(PACK)]
         z_planes = [keep.tile([P, T], F32, name="z_plane%d" % i, align_bytes=64) for i in range(PACK)]
         wa_raw = keep.tile([P, PACK, N], F32, name="wa_raw", align_bytes=64)
-        wb_raw = [keep.tile([P, PACK, N // 2], F32, name="wb_raw%d" % h) for h in range(2)]
+        wb_raw = keep.tile([P, PACK, N], F32, name="wb_raw")
         res_sb = keep.tile([P, N_TILES, J], F32, name="res_sb")
 
         x_rows = xT.rearrange("(p i) t -> p i t", i=PACK)
@@ -57,17 +59,19 @@ def tile_list_hl_gate_res_kernel(tc, xT, wgt, zT, wgt2, wa, wb, res, offs, offs2
         res_rows = res.rearrange("(t p) j -> p t j", p=P)
         out_rows = out.rearrange("(t p) j -> p t j", p=P)
 
-        for r in range(0, PACK, 2):
-            nc.sync.dma_start(out=wb_raw[0][:, r : r + 2, :], in_=wb_rows[:, r : r + 2, : N // 2])
-        nc.sync.dma_start(out=wb_raw[1][:], in_=wb_rows[:, :, N // 2 :])
+        z_wgt_rows = keep.tile([P, P], F32, name="z_wgt_rows")
+        nc.sync.dma_start(out=z_wgt_rows[:], in_=wgt2.rearrange("(a q) (r c) -> q a r c", q=8, c=P)[0])
+        wb_pieces = [slice(r0, r1) for r0, r1 in zip(WB_CUTS, WB_CUTS[1:])]
+        for rows in wb_pieces:
+            nc.sync.dma_start(out=wb_raw[:, rows, :], in_=wb_rows[:, rows, :])
         nc.sync.dma_start(z_offs[:], offs2)
         nc.sync.dma_start(out=z_planes[0][:], in_=z_rows[:, 0, :])
-        for h in range(2):
-            nc.sync.dma_start(out=z_wgt[:, h * (J // 2) : (h + 1) * (J // 2)], in_=wgt2[:, h * (J // 2) : (h + 1) * (J // 2)])
-        for i in range(1, PACK):
+        nc.sync.dma_start(out=z_planes[1][:], in_=z_rows[:, 1, :])
+        x_wgt_rows = keep.tile([P, P], F32, name="x_wgt_rows")
+        nc.sync.dma_start(out=x_wgt_rows[:], in_=wgt.rearrange("(a q) (r c) -> q a r c", q=8, c=P)[0])
+        for i in range(2, PACK):
             nc.sync.dma_start(out=z_planes[i][:], in_=z_rows[:, i, :])
         nc.sync.dma_start(x_offs[:], offs)
-        nc.sync.dma_start(out=x_wgt[:], in_=wgt)
         for i in range(2):
             nc.sync.dma_start(out=x_planes[i][:], in_=x_rows[:, i, :])
         nc.sync.dma_start(out=wa_raw[:], in_=wa.rearrange("(p i) n -> p i n", i=PACK))
@@ -84,9 +88,9 @@ def tile_list_hl_gate_res_kernel(tc, xT, wgt, zT, wgt2, wa, wb, res, offs, offs2
             quantize(nc, codes[:], scales[:], grouped[:])
             return codes, scales
 
-        def interleaved(name, sources):
+        def interleaved(name, sources, tag=None):
             width = sources[0].shape[2]
-            grouped = keep.tile([P, len(sources) * width, PACK], BF16, name="grouped_" + name, align_bytes=64)
+            grouped = keep.tile([P, len(sources) * width, PACK], BF16, name="grouped_" + name, tag=tag or "grouped_" + name, align_bytes=64)
             for s, src in enumerate(sources):
                 interleave(nc, grouped[:, s * width : (s + 1) * width, :], src)
             return grouped
@@ -103,36 +107,52 @@ def tile_list_hl_gate_res_kernel(tc, xT, wgt, zT, wgt2, wa, wb, res, offs, offs2
                 weight[:, cols], ALU.mult,
             )
 
-        wb_grouped = []
-        for h in range(2):
-            wb_hi = keep.tile([P, PACK, N // 2], F32, name="wb_hi%d" % h)
-            wb_lo = keep.tile([P, PACK, N // 2], BF16, name="wb_lo%d" % h)
-            step = 2 if h == 0 else PACK
-            for r in range(0, PACK, step):
-                rows = slice(r, r + step)
-                nc.vector.tensor_scalar(
-                    out=wb_hi[:, rows, :].bitcast(I32), in0=wb_raw[h][:, rows, :].bitcast(I32),
-                    scalar1=HI_MASK, scalar2=None, op0=ALU.bitwise_and,
-                )
-            for r in range(0, PACK, step):
-                rows = slice(r, r + step)
-                nc.vector.tensor_tensor(
-                    out=wb_lo[:, rows, :], in0=wb_raw[h][:, rows, :], in1=wb_hi[:, rows, :], op=ALU.subtract
-                )
-            wb_grouped.append(interleaved("wb%d" % h, [wb_hi[:], wb_lo[:]]))
+        identity = keep.tile([P, P], F32, name="identity")
+        make_identity(nc, identity[:])
 
-        wb_mx = [quantized("wb0", wb_grouped[0], "codes_wb0")]
+        def spread_weights(name, rows, weight):
+            turned = psum.tile([P, BANK], F32, name="ya")
+            nc.tensor.transpose(turned[:, :P], rows[:], identity[:])
+            spread = keep.tile([P, 8, 16, 8], F32, name="spread_" + name, align_bytes=64)
+            nc.scalar.copy(
+                out=spread[:],
+                in_=turned[:, :P].rearrange("c (a r) -> c r a", r=8).unsqueeze(3).to_broadcast([P, 8, 16, 8]),
+            )
+            for h in range(2):
+                back = psum.tile([P, 4, P], F32, name="ya")
+                for r in range(4):
+                    nc.tensor.transpose(
+                        back[:, r, :], spread[:, 4 * h + r, :, :].rearrange("c a q -> c (a q)"), identity[:]
+                    )
+                nc.scalar.copy(out=weight[:, h * BANK : (h + 1) * BANK], in_=back[:].rearrange("p r c -> p (r c)"))
+
+        spread_weights("z", z_wgt_rows, z_wgt)
+
+        wb_hi = keep.tile([P, PACK, N], F32, name="wb_hi")
+        wb_lo = keep.tile([P, PACK, N], BF16, name="wb_lo")
+        for rows in wb_pieces:
+            nc.vector.tensor_scalar(
+                out=wb_hi[:, rows, :].bitcast(I32), in0=wb_raw[:, rows, :].bitcast(I32),
+                scalar1=HI_MASK, scalar2=None, op0=ALU.bitwise_and,
+            )
+        for rows in wb_pieces:
+            nc.vector.tensor_tensor(
+                out=wb_lo[:, rows, :], in0=wb_raw[:, rows, :], in1=wb_hi[:, rows, :], op=ALU.subtract
+            )
+        wb_grouped = interleaved("wb", [wb_hi[:], wb_lo[:]], "spread_z")
+        spread_weights("x", x_wgt_rows, x_wgt)
+
         z_picked = keep.tile([P, PACK, J], F32, name="picked_z")
-        for i, width in enumerate((J // 2, J, J, J // 2)):
+        for i, width in enumerate((J, J, J, J // 2)):
             for c0 in range(0, J, width):
                 gather(z_picked[:, i, :], z_planes[i], z_offs, z_wgt, slice(c0, c0 + width))
-        wb_mx.append(quantized("wb1", wb_grouped[1], "codes_wb1"))
-        z_grouped = [interleaved("z%d" % h, [z_picked[:, :, h * (J // 2) : (h + 1) * (J // 2)]]) for h in range(2)]
+        wb_mx = quantized("wb", wb_grouped, "z_plane1")
+        z_grouped = interleaved("z", [z_picked[:, :, h * (J // 2) : (h + 1) * (J // 2)] for h in range(2)], "spread_x")
         x_picked = keep.tile([P, PACK, J], F32, name="picked_x", align_bytes=64)
         for i in range(PACK - 1):
             gather(x_picked[:, i, :], x_planes[i], x_offs, x_wgt, slice(0, J))
 
-        z_mx = [quantized("z%d" % h, z_grouped[h], "x_plane%d" % h) for h in range(2)]
+        z_mx = [quantized("z%d" % h, z_grouped[:, h * (J // 2) : (h + 1) * (J // 2), :], "x_plane%d" % h) for h in range(2)]
 
         gates = {}
 
@@ -141,14 +161,13 @@ def tile_list_hl_gate_res_kernel(tc, xT, wgt, zT, wgt2, wa, wb, res, offs, offs2
             for e, half in enumerate(halves):
                 for u in range(2):
                     bank = psum.tile([P, J // 2], F32, name="yb")
-                    product(bank[:], wb_mx[half], u * P, z_mx[h], True, False)
-                    product(bank[:], wb_mx[half], N // 2 + u * P, z_mx[h], False, True)
+                    product(bank[:], wb_mx, (2 * half + u) * P, z_mx[h], True, False)
+                    product(bank[:], wb_mx, N + (2 * half + u) * P, z_mx[h], False, True)
                     nc.scalar.activation(out=gate[:, 2 * e + u, :], in_=bank[:], func=ACT.Sigmoid)
                 gates[h, half] = gate[:, 2 * e : 2 * e + 2, :]
 
         wa_grouped = interleaved("wa", [wa_raw[:]])
         gate_rows(0, (0, 1), "wa_raw")
-        gate_rows(1, (0,), "gate10")
 
         chunks = [slice(c0, c1) for c0, c1 in zip(X_CUTS, X_CUTS[1:])]
         x_grouped = []
@@ -157,29 +176,29 @@ def tile_list_hl_gate_res_kernel(tc, xT, wgt, zT, wgt2, wa, wb, res, offs, offs2
             x_grouped.append(interleaved("x%d" % c, [x_picked[:, :, cols]]))
         wa_mx = quantized("wa", wa_grouped, "x_plane3")
         x_mx = [quantized("x%d" % c, grouped, "codes_x%d" % c) for c, grouped in enumerate(x_grouped)]
-        gate_rows(1, (1,), "picked_x")
+        gate_rows(1, (0, 1), "picked_x")
 
-        pieces = []
+        gated = [keep.tile([P, N_TILES, J // 2], F32, name="gated%d" % h) for h in range(2)]
         for c, cols in enumerate(chunks):
             width = cols.stop - cols.start
-            for t0 in range(0, N_TILES, BANK // width):
-                rows = slice(t0, t0 + BANK // width)
-                bank = psum.tile([P, BANK // width, width], F32, name="ya")
-                for u in range(BANK // width):
-                    product(bank[:, u, :], wa_mx, (t0 + u) * P, x_mx[c], True, True)
-                gated = keep.tile([P, BANK // width, width], F32, name="gated%d_%d" % (c, t0))
-                h, c0 = divmod(cols.start, J // 2)
-                assert c0 + width <= J // 2
-                nc.vector.tensor_tensor(out=gated[:], in0=bank[:], in1=gates[h, t0 // 2][:, :, c0 : c0 + width], op=ALU.mult)
-                pieces.append((gated, rows, cols))
+            h, c0 = divmod(cols.start, J // 2)
+            for half in range(2):
+                bank = psum.tile([P, 2, width], F32, name="ya")
+                for u in range(2):
+                    product(bank[:, u, :], wa_mx, (2 * half + u) * P, x_mx[c], True, True)
+                nc.vector.tensor_tensor(
+                    out=gated[h][:, 2 * half : 2 * half + 2, c0 : c0 + width], in0=bank[:],
+                    in1=gates[h, half][:, :, c0 : c0 + width], op=ALU.mult,
+                )
 
         first = keep.tile([P, GPSIMD_PIECES, BANK], F32, name="first", tag="grouped_x%d" % (len(chunks) - 1), align_bytes=64)
-        for e, (gated, rows, cols) in enumerate(pieces):
+        for e in range(2 * N_TILES):
+            h, t = divmod(e, N_TILES)
+            cols = slice(h * (J // 2), (h + 1) * (J // 2))
             if e < GPSIMD_PIECES:
-                result = first[:, e, :].rearrange("p (u j) -> p u j", u=rows.stop - rows.start)
-                nc.gpsimd.tensor_tensor(out=result, in0=gated[:], in1=res_sb[:, rows, cols], op=ALU.add)
-                nc.scalar.dma_start(out=out_rows[:, rows, cols], in_=result)
+                nc.gpsimd.tensor_tensor(out=first[:, e, :], in0=gated[h][:, t, :], in1=res_sb[:, t, cols], op=ALU.add)
+                nc.scalar.dma_start(out=out_rows[:, t, cols], in_=first[:, e, :])
             else:
-                result = keep.tile(gated.shape, F32, name="result%d" % e)
-                nc.vector.tensor_tensor(out=result[:], in0=gated[:], in1=res_sb[:, rows, cols], op=ALU.add)
-                nc.sync.dma_start(out=out_rows[:, rows, cols], in_=result[:])
+                result = keep.tile([P, J // 2], F32, name="result%d" % e)
+                nc.vector.tensor_tensor(out=result[:], in0=gated[h][:, t, :], in1=res_sb[:, t, cols], op=ALU.add)
+                nc.sync.dma_start(out=out_rows[:, t, cols], in_=result[:])

@@ -18,23 +18,24 @@ ACT = mybir.ActivationFunctionType
 
 P = 128
 PACK = 4
+LIST_ROWS = 16
 N_TILES = N // P
-X_CUTS = (0, 256, 512, 768, 1024)
 BANK = 512
-WB_CUTS = (0, 1, 2, 3, 4)
-GPSIMD_PIECES = 2
+HALF = J // 2
+CHUNK = 256
+CHUNKS = J // CHUNK
+LINE = 4
 HI_MASK = -(1 << 20)
+WGT_PIECES = J // P
+WGT_ROWS = P // WGT_PIECES
+GPSIMD_STRIPS = 2
 
 
 def interleave(nc, dst, src):
     nc.scalar.copy(
-        out=dst.rearrange("p (c e) i -> p c i e", e=4),
-        in_=src.rearrange("p i (c e) -> p c i e", e=4),
+        out=dst.rearrange("p (c e) i -> p c i e", e=LINE),
+        in_=src.rearrange("p i (c e) -> p c i e", e=LINE),
     )
-
-
-def quantize(nc, codes, scales, grouped):
-    nc.vector.quantize_mx(out=codes.bitcast(FP8X4), scales=scales, in_=grouped.rearrange("p c i -> p (c i)"))
 
 
 def tile_list_hl_gate_res_kernel(tc, xT, wgt, zT, wgt2, wa, wb, res, offs, offs2, out):
@@ -43,8 +44,8 @@ def tile_list_hl_gate_res_kernel(tc, xT, wgt, zT, wgt2, wa, wb, res, offs, offs2
         keep = ctx.enter_context(tc.tile_pool(name="keep", bufs=1))
         psum = ctx.enter_context(tc.psum_pool(name="psum", bufs=4))
 
-        x_offs = keep.tile([P, J // 16], U16, name="x_offs")
-        z_offs = keep.tile([P, J // 16], U16, name="z_offs")
+        x_offs = keep.tile([P, J // LIST_ROWS], U16, name="x_offs")
+        z_offs = keep.tile([P, J // LIST_ROWS], U16, name="z_offs")
         x_wgt = keep.tile([P, J], F32, name="x_wgt", align_bytes=64)
         z_wgt = keep.tile([P, J], F32, name="z_wgt")
         x_planes = [keep.tile([P, T], F32, name="x_plane%d" % i, align_bytes=64) for i in range(PACK)]
@@ -58,17 +59,20 @@ def tile_list_hl_gate_res_kernel(tc, xT, wgt, zT, wgt2, wa, wb, res, offs, offs2
         wb_rows = wb.rearrange("(p i) n -> p i n", i=PACK)
         res_rows = res.rearrange("(t p) j -> p t j", p=P)
         out_rows = out.rearrange("(t p) j -> p t j", p=P)
+        halves = [slice(h * HALF, (h + 1) * HALF) for h in range(2)]
 
-        z_wgt_rows = keep.tile([P, P], F32, name="z_wgt_rows")
-        nc.sync.dma_start(out=z_wgt_rows[:], in_=wgt2.rearrange("(a q) (r c) -> q a r c", q=8, c=P)[0])
-        wb_pieces = [slice(r0, r1) for r0, r1 in zip(WB_CUTS, WB_CUTS[1:])]
-        for rows in wb_pieces:
-            nc.sync.dma_start(out=wb_raw[:, rows, :], in_=wb_rows[:, rows, :])
+        def load_weight_pieces(name, weights):
+            pieces = keep.tile([P, P], F32, name=name)
+            nc.sync.dma_start(out=pieces[:], in_=weights.rearrange("(a q) (r c) -> q a r c", q=WGT_PIECES, c=P)[0])
+            return pieces
+
+        z_wgt_pieces = load_weight_pieces("z_wgt_rows", wgt2)
+        for i in range(PACK):
+            nc.sync.dma_start(out=wb_raw[:, i : i + 1, :], in_=wb_rows[:, i : i + 1, :])
         nc.sync.dma_start(z_offs[:], offs2)
-        nc.sync.dma_start(out=z_planes[0][:], in_=z_rows[:, 0, :])
-        nc.sync.dma_start(out=z_planes[1][:], in_=z_rows[:, 1, :])
-        x_wgt_rows = keep.tile([P, P], F32, name="x_wgt_rows")
-        nc.sync.dma_start(out=x_wgt_rows[:], in_=wgt.rearrange("(a q) (r c) -> q a r c", q=8, c=P)[0])
+        for i in range(2):
+            nc.sync.dma_start(out=z_planes[i][:], in_=z_rows[:, i, :])
+        x_wgt_pieces = load_weight_pieces("x_wgt_rows", wgt)
         for i in range(2, PACK):
             nc.sync.dma_start(out=z_planes[i][:], in_=z_rows[:, i, :])
         nc.sync.dma_start(x_offs[:], offs)
@@ -77,128 +81,149 @@ def tile_list_hl_gate_res_kernel(tc, xT, wgt, zT, wgt2, wa, wb, res, offs, offs2
         nc.sync.dma_start(out=wa_raw[:], in_=wa.rearrange("(p i) n -> p i n", i=PACK))
         for i in range(2, PACK):
             nc.sync.dma_start(out=x_planes[i][:], in_=x_rows[:, i, :])
-        for h in range(2):
-            cols = slice(h * (J // 2), (h + 1) * (J // 2))
+        for cols in halves:
             nc.sync.dma_start(out=res_sb[:, :, cols], in_=res_rows[:, :, cols])
 
         def quantized(name, grouped, tag):
             width = grouped.shape[1]
             codes = keep.tile([P, width], U32, name="codes_" + name, tag=tag, align_bytes=64)
             scales = keep.tile([P, width], U8, name="scales_" + name, align_bytes=64)
-            quantize(nc, codes[:], scales[:], grouped[:])
+            nc.vector.quantize_mx(
+                out=codes[:].bitcast(FP8X4), scales=scales[:], in_=grouped[:].rearrange("p c i -> p (c i)")
+            )
             return codes, scales
 
-        def interleaved(name, sources, tag=None):
+        def interleaved(name, sources, tag):
             width = sources[0].shape[2]
-            grouped = keep.tile([P, len(sources) * width, PACK], BF16, name="grouped_" + name, tag=tag or "grouped_" + name, align_bytes=64)
+            grouped = keep.tile([P, len(sources) * width, PACK], BF16, name="grouped_" + name, tag=tag, align_bytes=64)
             for s, src in enumerate(sources):
                 interleave(nc, grouped[:, s * width : (s + 1) * width, :], src)
             return grouped
 
-        def product(bank, weight, col, moving, start, stop):
+        def product(bank, weight_mx, col, moving_mx, start, stop):
             nc.tensor.matmul_mx(
-                out=bank, lhsT=weight[0][:, col : col + P].bitcast(FP8X4), lhsT_scale=weight[1][:, col : col + P],
-                rhs=moving[0][:].bitcast(FP8X4), rhs_scale=moving[1][:], start=start, stop=stop,
+                out=bank,
+                lhsT=weight_mx[0][:, col : col + P].bitcast(FP8X4),
+                lhsT_scale=weight_mx[1][:, col : col + P],
+                rhs=moving_mx[0][:].bitcast(FP8X4),
+                rhs_scale=moving_mx[1][:],
+                start=start,
+                stop=stop,
             )
 
         def gather(values, plane, offsets, weight, cols):
             nc.vector.tensor_tensor(
-                values[:, cols], plane[:].indirect(offsets[:, cols.start // 16 : cols.stop // 16]),
-                weight[:, cols], ALU.mult,
+                values[:, cols],
+                plane[:].indirect(offsets[:, cols.start // LIST_ROWS : cols.stop // LIST_ROWS]),
+                weight[:, cols],
+                ALU.mult,
             )
 
         identity = keep.tile([P, P], F32, name="identity")
         make_identity(nc, identity[:])
 
-        def spread_weights(name, rows, weight):
+        def spread_weights(name, pieces, weight):
             turned = psum.tile([P, BANK], F32, name="ya")
-            nc.tensor.transpose(turned[:, :P], rows[:], identity[:])
-            spread = keep.tile([P, 8, 16, 8], F32, name="spread_" + name, align_bytes=64)
-            nc.scalar.copy(
-                out=spread[:],
-                in_=turned[:, :P].rearrange("c (a r) -> c r a", r=8).unsqueeze(3).to_broadcast([P, 8, 16, 8]),
-            )
+            nc.tensor.transpose(turned[:, :P], pieces[:], identity[:])
+            spread = keep.tile([P, WGT_PIECES, WGT_ROWS, WGT_PIECES], F32, name="spread_" + name, align_bytes=64)
+            by_piece = turned[:, :P].rearrange("c (a r) -> c r a", r=WGT_PIECES)
+            per_bank = BANK // P
             for h in range(2):
-                back = psum.tile([P, 4, P], F32, name="ya")
-                for r in range(4):
+                nc.scalar.copy(
+                    out=spread[:, per_bank * h : per_bank * (h + 1), :, :],
+                    in_=by_piece[:, per_bank * h : per_bank * (h + 1), :]
+                    .unsqueeze(3)
+                    .to_broadcast([P, per_bank, WGT_ROWS, WGT_PIECES]),
+                )
+            for h in range(2):
+                back = psum.tile([P, per_bank, P], F32, name="ya")
+                for r in range(per_bank):
                     nc.tensor.transpose(
-                        back[:, r, :], spread[:, 4 * h + r, :, :].rearrange("c a q -> c (a q)"), identity[:]
+                        back[:, r, :], spread[:, per_bank * h + r, :, :].rearrange("c a q -> c (a q)"), identity[:]
                     )
-                nc.scalar.copy(out=weight[:, h * BANK : (h + 1) * BANK], in_=back[:].rearrange("p r c -> p (r c)"))
+                nc.scalar.copy(out=weight[:, halves[h]], in_=back[:].rearrange("p r c -> p (r c)"))
 
-        spread_weights("z", z_wgt_rows, z_wgt)
+        spread_weights("z", z_wgt_pieces, z_wgt)
 
         wb_hi = keep.tile([P, PACK, N], F32, name="wb_hi")
         wb_lo = keep.tile([P, PACK, N], BF16, name="wb_lo")
-        for rows in wb_pieces:
+        for i in range(PACK):
             nc.vector.tensor_scalar(
-                out=wb_hi[:, rows, :].bitcast(I32), in0=wb_raw[:, rows, :].bitcast(I32),
-                scalar1=HI_MASK, scalar2=None, op0=ALU.bitwise_and,
+                out=wb_hi[:, i : i + 1, :].bitcast(I32),
+                in0=wb_raw[:, i : i + 1, :].bitcast(I32),
+                scalar1=HI_MASK,
+                scalar2=None,
+                op0=ALU.bitwise_and,
             )
-        for rows in wb_pieces:
+        for i in range(PACK):
             nc.vector.tensor_tensor(
-                out=wb_lo[:, rows, :], in0=wb_raw[:, rows, :], in1=wb_hi[:, rows, :], op=ALU.subtract
+                out=wb_lo[:, i : i + 1, :], in0=wb_raw[:, i : i + 1, :], in1=wb_hi[:, i : i + 1, :], op=ALU.subtract
             )
         wb_grouped = interleaved("wb", [wb_hi[:], wb_lo[:]], "spread_z")
-        spread_weights("x", x_wgt_rows, x_wgt)
+        spread_weights("x", x_wgt_pieces, x_wgt)
 
         z_picked = keep.tile([P, PACK, J], F32, name="picked_z")
-        for i, width in enumerate((J, J, J, J // 2)):
-            for c0 in range(0, J, width):
-                gather(z_picked[:, i, :], z_planes[i], z_offs, z_wgt, slice(c0, c0 + width))
+        for i in range(PACK - 1):
+            gather(z_picked[:, i, :], z_planes[i], z_offs, z_wgt, slice(0, J))
+        for cols in halves:
+            gather(z_picked[:, PACK - 1, :], z_planes[PACK - 1], z_offs, z_wgt, cols)
         wb_mx = quantized("wb", wb_grouped, "z_plane1")
-        z_grouped = interleaved("z", [z_picked[:, :, h * (J // 2) : (h + 1) * (J // 2)] for h in range(2)], "spread_x")
+        z_grouped = interleaved("z", [z_picked[:, :, cols] for cols in halves], "spread_x")
+
         x_picked = keep.tile([P, PACK, J], F32, name="picked_x", align_bytes=64)
         for i in range(PACK - 1):
             gather(x_picked[:, i, :], x_planes[i], x_offs, x_wgt, slice(0, J))
 
-        z_mx = [quantized("z%d" % h, z_grouped[:, h * (J // 2) : (h + 1) * (J // 2), :], "x_plane%d" % h) for h in range(2)]
+        z_mx = [quantized("z%d" % h, z_grouped[:, halves[h], :], "x_plane%d" % h) for h in range(2)]
 
-        gates = {}
+        def gate_half(h, tag):
+            gate = keep.tile([P, N_TILES, HALF], F32, name="gate%d0" % h, tag=tag, align_bytes=64)
+            for t in range(N_TILES):
+                bank = psum.tile([P, HALF], F32, name="yb")
+                product(bank[:], wb_mx, t * P, z_mx[h], True, False)
+                product(bank[:], wb_mx, N + t * P, z_mx[h], False, True)
+                nc.scalar.activation(out=gate[:, t, :], in_=bank[:], func=ACT.Sigmoid)
+            return gate
 
-        def gate_rows(h, halves, tag):
-            gate = keep.tile([P, 2 * len(halves), J // 2], F32, name="gate%d%d" % (h, halves[0]), tag=tag, align_bytes=64)
-            for e, half in enumerate(halves):
-                for u in range(2):
-                    bank = psum.tile([P, J // 2], F32, name="yb")
-                    product(bank[:], wb_mx, (2 * half + u) * P, z_mx[h], True, False)
-                    product(bank[:], wb_mx, N + (2 * half + u) * P, z_mx[h], False, True)
-                    nc.scalar.activation(out=gate[:, 2 * e + u, :], in_=bank[:], func=ACT.Sigmoid)
-                gates[h, half] = gate[:, 2 * e : 2 * e + 2, :]
+        wa_grouped = interleaved("wa", [wa_raw[:]], "grouped_wa")
+        gates = [gate_half(0, "wa_raw")]
 
-        wa_grouped = interleaved("wa", [wa_raw[:]])
-        gate_rows(0, (0, 1), "wa_raw")
-
-        chunks = [slice(c0, c1) for c0, c1 in zip(X_CUTS, X_CUTS[1:])]
+        chunks = [slice(c * CHUNK, (c + 1) * CHUNK) for c in range(CHUNKS)]
         x_grouped = []
         for c, cols in enumerate(chunks):
             gather(x_picked[:, PACK - 1, :], x_planes[PACK - 1], x_offs, x_wgt, cols)
-            x_grouped.append(interleaved("x%d" % c, [x_picked[:, :, cols]]))
-        wa_mx = quantized("wa", wa_grouped, "x_plane3")
+            x_grouped.append(interleaved("x%d" % c, [x_picked[:, :, cols]], "grouped_x%d" % c))
+        wa_mx = quantized("wa", wa_grouped, "x_plane%d" % (PACK - 1))
         x_mx = [quantized("x%d" % c, grouped, "codes_x%d" % c) for c, grouped in enumerate(x_grouped)]
-        gate_rows(1, (0, 1), "picked_x")
+        gates.append(gate_half(1, "picked_x"))
 
-        gated = [keep.tile([P, N_TILES, J // 2], F32, name="gated%d" % h) for h in range(2)]
-        for c, cols in enumerate(chunks):
-            width = cols.stop - cols.start
-            h, c0 = divmod(cols.start, J // 2)
-            for half in range(2):
-                bank = psum.tile([P, 2, width], F32, name="ya")
-                for u in range(2):
-                    product(bank[:, u, :], wa_mx, (2 * half + u) * P, x_mx[c], True, True)
+        tiles_per_bank = BANK // CHUNK
+        gated = [keep.tile([P, N_TILES, HALF], F32, name="gated%d" % h) for h in range(2)]
+        for c in range(CHUNKS):
+            h, c0 = divmod(c * CHUNK, HALF)
+            for t0 in range(0, N_TILES, tiles_per_bank):
+                tiles = slice(t0, t0 + tiles_per_bank)
+                bank = psum.tile([P, tiles_per_bank, CHUNK], F32, name="ya")
+                for u in range(tiles_per_bank):
+                    product(bank[:, u, :], wa_mx, (t0 + u) * P, x_mx[c], True, True)
                 nc.vector.tensor_tensor(
-                    out=gated[h][:, 2 * half : 2 * half + 2, c0 : c0 + width], in0=bank[:],
-                    in1=gates[h, half][:, :, c0 : c0 + width], op=ALU.mult,
+                    out=gated[h][:, tiles, c0 : c0 + CHUNK],
+                    in0=bank[:],
+                    in1=gates[h][:, tiles, c0 : c0 + CHUNK],
+                    op=ALU.mult,
                 )
 
-        first = keep.tile([P, GPSIMD_PIECES, BANK], F32, name="first", tag="grouped_x%d" % (len(chunks) - 1), align_bytes=64)
-        for e in range(2 * N_TILES):
-            h, t = divmod(e, N_TILES)
-            cols = slice(h * (J // 2), (h + 1) * (J // 2))
-            if e < GPSIMD_PIECES:
-                nc.gpsimd.tensor_tensor(out=first[:, e, :], in0=gated[h][:, t, :], in1=res_sb[:, t, cols], op=ALU.add)
-                nc.scalar.dma_start(out=out_rows[:, t, cols], in_=first[:, e, :])
+        gpsimd_sums = keep.tile(
+            [P, GPSIMD_STRIPS, HALF], F32, name="first", tag="grouped_x%d" % (CHUNKS - 1), align_bytes=64
+        )
+        for strip in range(2 * N_TILES):
+            h, t = divmod(strip, N_TILES)
+            if strip < GPSIMD_STRIPS:
+                nc.gpsimd.tensor_tensor(
+                    out=gpsimd_sums[:, strip, :], in0=gated[h][:, t, :], in1=res_sb[:, t, halves[h]], op=ALU.add
+                )
+                nc.scalar.dma_start(out=out_rows[:, t, halves[h]], in_=gpsimd_sums[:, strip, :])
             else:
-                result = keep.tile([P, J // 2], F32, name="result%d" % e)
-                nc.vector.tensor_tensor(out=result[:], in0=gated[h][:, t, :], in1=res_sb[:, t, cols], op=ALU.add)
-                nc.sync.dma_start(out=out_rows[:, t, cols], in_=result[:])
+                result = keep.tile([P, HALF], F32, name="result%d" % strip)
+                nc.vector.tensor_tensor(out=result[:], in0=gated[h][:, t, :], in1=res_sb[:, t, halves[h]], op=ALU.add)
+                nc.sync.dma_start(out=out_rows[:, t, halves[h]], in_=result[:])

from contextlib import ExitStack

import concourse.mybir as mybir
from concourse.masks import make_identity

K, L, N, T, J = 512, 512, 512, 2048, 1024
FLOPS = 2 * N * J * (K + 2 * L)

F32 = mybir.dt.float32
BF16 = mybir.dt.bfloat16
I32 = mybir.dt.int32
U32 = mybir.dt.uint32
U16 = mybir.dt.uint16
U8 = mybir.dt.uint8
FP8X4 = mybir.dt.float8_e4m3fn_x4
ALU = mybir.AluOpType
ACT = mybir.ActivationFunctionType

P = 128
PACK = 4
LIST_ROWS = 16
N_TILES = N // P
BANK = 512
HALF = J // 2
CHUNK = 256
CHUNKS = J // CHUNK
LINE = 4
HI_MASK = -(1 << 20)
WGT_PIECES = J // P
WGT_ROWS = P // WGT_PIECES
GPSIMD_STRIPS = 2


def interleave(nc, dst, src):
    nc.scalar.copy(
        out=dst.rearrange("p (c e) i -> p c i e", e=LINE),
        in_=src.rearrange("p i (c e) -> p c i e", e=LINE),
    )


def tile_list_hl_gate_res_kernel(tc, xT, wgt, zT, wgt2, wa, wb, res, offs, offs2, out):
    nc = tc.nc
    with ExitStack() as ctx:
        keep = ctx.enter_context(tc.tile_pool(name="keep", bufs=1))
        psum = ctx.enter_context(tc.psum_pool(name="psum", bufs=4))

        x_offs = keep.tile([P, J // LIST_ROWS], U16, name="x_offs")
        z_offs = keep.tile([P, J // LIST_ROWS], U16, name="z_offs")
        x_wgt = keep.tile([P, J], F32, name="x_wgt", align_bytes=64)
        z_wgt = keep.tile([P, J], F32, name="z_wgt")
        x_planes = [keep.tile([P, T], F32, name="x_plane%d" % i, align_bytes=64) for i in range(PACK)]
        z_planes = [keep.tile([P, T], F32, name="z_plane%d" % i, align_bytes=64) for i in range(PACK)]
        wa_raw = keep.tile([P, PACK, N], F32, name="wa_raw", align_bytes=64)
        wb_raw = keep.tile([P, PACK, N], F32, name="wb_raw")
        res_sb = keep.tile([P, N_TILES, J], F32, name="res_sb")

        x_rows = xT.rearrange("(p i) t -> p i t", i=PACK)
        z_rows = zT.rearrange("(p i) t -> p i t", i=PACK)
        wb_rows = wb.rearrange("(p i) n -> p i n", i=PACK)
        res_rows = res.rearrange("(t p) j -> p t j", p=P)
        out_rows = out.rearrange("(t p) j -> p t j", p=P)
        halves = [slice(h * HALF, (h + 1) * HALF) for h in range(2)]

        def load_weight_pieces(name, weights):
            pieces = keep.tile([P, P], F32, name=name)
            nc.sync.dma_start(out=pieces[:], in_=weights.rearrange("(a q) (r c) -> q a r c", q=WGT_PIECES, c=P)[0])
            return pieces

        z_wgt_pieces = load_weight_pieces("z_wgt_rows", wgt2)
        for i in range(PACK):
            nc.sync.dma_start(out=wb_raw[:, i : i + 1, :], in_=wb_rows[:, i : i + 1, :])
        nc.sync.dma_start(z_offs[:], offs2)
        for i in range(2):
            nc.sync.dma_start(out=z_planes[i][:], in_=z_rows[:, i, :])
        x_wgt_pieces = load_weight_pieces("x_wgt_rows", wgt)
        for i in range(2, PACK):
            nc.sync.dma_start(out=z_planes[i][:], in_=z_rows[:, i, :])
        nc.sync.dma_start(x_offs[:], offs)
        for i in range(2):
            nc.sync.dma_start(out=x_planes[i][:], in_=x_rows[:, i, :])
        nc.sync.dma_start(out=wa_raw[:], in_=wa.rearrange("(p i) n -> p i n", i=PACK))
        for i in range(2, PACK):
            nc.sync.dma_start(out=x_planes[i][:], in_=x_rows[:, i, :])
        for cols in halves:
            nc.sync.dma_start(out=res_sb[:, :, cols], in_=res_rows[:, :, cols])

        def quantized(name, grouped, tag):
            width = grouped.shape[1]
            codes = keep.tile([P, width], U32, name="codes_" + name, tag=tag, align_bytes=64)
            scales = keep.tile([P, width], U8, name="scales_" + name, align_bytes=64)
            nc.vector.quantize_mx(
                out=codes[:].bitcast(FP8X4), scales=scales[:], in_=grouped[:].rearrange("p c i -> p (c i)")
            )
            return codes, scales

        def interleaved(name, sources, tag):
            width = sources[0].shape[2]
            grouped = keep.tile([P, len(sources) * width, PACK], BF16, name="grouped_" + name, tag=tag, align_bytes=64)
            for s, src in enumerate(sources):
                interleave(nc, grouped[:, s * width : (s + 1) * width, :], src)
            return grouped

        def product(bank, weight_mx, col, moving_mx, start, stop):
            nc.tensor.matmul_mx(
                out=bank,
                lhsT=weight_mx[0][:, col : col + P].bitcast(FP8X4),
                lhsT_scale=weight_mx[1][:, col : col + P],
                rhs=moving_mx[0][:].bitcast(FP8X4),
                rhs_scale=moving_mx[1][:],
                start=start,
                stop=stop,
            )

        def gather(values, plane, offsets, weight, cols):
            nc.vector.tensor_tensor(
                values[:, cols],
                plane[:].indirect(offsets[:, cols.start // LIST_ROWS : cols.stop // LIST_ROWS]),
                weight[:, cols],
                ALU.mult,
            )

        identity = keep.tile([P, P], F32, name="identity")
        make_identity(nc, identity[:])

        def spread_weights(name, pieces, weight):
            turned = psum.tile([P, BANK], F32, name="ya")
            nc.tensor.transpose(turned[:, :P], pieces[:], identity[:])
            spread = keep.tile([P, WGT_PIECES, WGT_ROWS, WGT_PIECES], F32, name="spread_" + name, align_bytes=64)
            by_piece = turned[:, :P].rearrange("c (a r) -> c r a", r=WGT_PIECES)
            per_bank = BANK // P
            for h in range(2):
                nc.scalar.copy(
                    out=spread[:, per_bank * h : per_bank * (h + 1), :, :],
                    in_=by_piece[:, per_bank * h : per_bank * (h + 1), :]
                    .unsqueeze(3)
                    .to_broadcast([P, per_bank, WGT_ROWS, WGT_PIECES]),
                )
            for h in range(2):
                back = psum.tile([P, per_bank, P], F32, name="ya")
                for r in range(per_bank):
                    nc.tensor.transpose(
                        back[:, r, :], spread[:, per_bank * h + r, :, :].rearrange("c a q -> c (a q)"), identity[:]
                    )
                nc.scalar.copy(out=weight[:, halves[h]], in_=back[:].rearrange("p r c -> p (r c)"))

        spread_weights("z", z_wgt_pieces, z_wgt)

        wb_hi = keep.tile([P, PACK, N], F32, name="wb_hi")
        wb_lo = keep.tile([P, PACK, N], BF16, name="wb_lo")
        for i in range(PACK):
            nc.vector.tensor_scalar(
                out=wb_hi[:, i : i + 1, :].bitcast(I32),
                in0=wb_raw[:, i : i + 1, :].bitcast(I32),
                scalar1=HI_MASK,
                scalar2=None,
                op0=ALU.bitwise_and,
            )
        for i in range(PACK):
            nc.vector.tensor_tensor(
                out=wb_lo[:, i : i + 1, :], in0=wb_raw[:, i : i + 1, :], in1=wb_hi[:, i : i + 1, :], op=ALU.subtract
            )
        wb_grouped = interleaved("wb", [wb_hi[:], wb_lo[:]], "spread_z")
        spread_weights("x", x_wgt_pieces, x_wgt)

        z_picked = keep.tile([P, PACK, J], F32, name="picked_z")
        for i in range(PACK - 1):
            gather(z_picked[:, i, :], z_planes[i], z_offs, z_wgt, slice(0, J))
        for cols in halves:
            gather(z_picked[:, PACK - 1, :], z_planes[PACK - 1], z_offs, z_wgt, cols)
        wb_mx = quantized("wb", wb_grouped, "z_plane1")
        z_grouped = interleaved("z", [z_picked[:, :, cols] for cols in halves], "spread_x")

        x_picked = keep.tile([P, PACK, J], F32, name="picked_x", align_bytes=64)
        for i in range(PACK - 1):
            gather(x_picked[:, i, :], x_planes[i], x_offs, x_wgt, slice(0, J))

        z_mx = [quantized("z%d" % h, z_grouped[:, halves[h], :], "x_plane%d" % h) for h in range(2)]

        def gate_half(h, tag):
            gate = keep.tile([P, N_TILES, HALF], F32, name="gate%d0" % h, tag=tag, align_bytes=64)
            for t in range(N_TILES):
                bank = psum.tile([P, HALF], F32, name="yb")
                product(bank[:], wb_mx, t * P, z_mx[h], True, False)
                product(bank[:], wb_mx, N + t * P, z_mx[h], False, True)
                nc.scalar.activation(out=gate[:, t, :], in_=bank[:], func=ACT.Sigmoid)
            return gate

        wa_grouped = interleaved("wa", [wa_raw[:]], "grouped_wa")
        gates = [gate_half(0, "wa_raw")]

        chunks = [slice(c * CHUNK, (c + 1) * CHUNK) for c in range(CHUNKS)]
        x_grouped = []
        for c, cols in enumerate(chunks):
            gather(x_picked[:, PACK - 1, :], x_planes[PACK - 1], x_offs, x_wgt, cols)
            x_grouped.append(interleaved("x%d" % c, [x_picked[:, :, cols]], "grouped_x%d" % c))
        wa_mx = quantized("wa", wa_grouped, "x_plane%d" % (PACK - 1))
        x_mx = [quantized("x%d" % c, grouped, "codes_x%d" % c) for c, grouped in enumerate(x_grouped)]
        gates.append(gate_half(1, "picked_x"))

        tiles_per_bank = BANK // CHUNK
        gated = [keep.tile([P, N_TILES, HALF], F32, name="gated%d" % h) for h in range(2)]
        for c in range(CHUNKS):
            h, c0 = divmod(c * CHUNK, HALF)
            for t0 in range(0, N_TILES, tiles_per_bank):
                tiles = slice(t0, t0 + tiles_per_bank)
                bank = psum.tile([P, tiles_per_bank, CHUNK], F32, name="ya")
                for u in range(tiles_per_bank):
                    product(bank[:, u, :], wa_mx, (t0 + u) * P, x_mx[c], True, True)
                nc.vector.tensor_tensor(
                    out=gated[h][:, tiles, c0 : c0 + CHUNK],
                    in0=bank[:],
                    in1=gates[h][:, tiles, c0 : c0 + CHUNK],
                    op=ALU.mult,
                )

        gpsimd_sums = keep.tile(
            [P, GPSIMD_STRIPS, HALF], F32, name="first", tag="grouped_x%d" % (CHUNKS - 1), align_bytes=64
        )
        for strip in range(2 * N_TILES):
            h, t = divmod(strip, N_TILES)
            if strip < GPSIMD_STRIPS:
                nc.gpsimd.tensor_tensor(
                    out=gpsimd_sums[:, strip, :], in0=gated[h][:, t, :], in1=res_sb[:, t, halves[h]], op=ALU.add
                )
                nc.scalar.dma_start(out=out_rows[:, t, halves[h]], in_=gpsimd_sums[:, strip, :])
            else:
                result = keep.tile([P, HALF], F32, name="result%d" % strip)
                nc.vector.tensor_tensor(out=result[:], in0=gated[h][:, t, :], in1=res_sb[:, t, halves[h]], op=ALU.add)
                nc.sync.dma_start(out=out_rows[:, t, halves[h]], in_=result[:])
